import numpy as np, ml_dtypes
CORES = [40,64,80,88,96,104,120,144]
N = 8
BF = ml_dtypes.bfloat16
def gentries(a):
    return np.ascontiguousarray(a.reshape(8, 16, -1).transpose(0, 2, 1)).reshape(8, -1)
def gtable(e):
    e = np.asarray(e); return np.ascontiguousarray(e.reshape(8, -1, 16).transpose(0, 2, 1)).reshape(128, -1).astype(np.int32)
R0, P0, S, L, RO = 3584, 288, 16, 12, 2
P = P0 + RO * S; R = R0 + RO * (N - 1) * S
def counts(rng, share):
    return np.where(rng.random((N, 8, P0)) < share, rng.integers(L, 17, (N, 8, P0)), rng.integers(1, L, (N, 8, P0)))
def world(rng, cnt):
    post = rng.integers(0, R0, (N, 8, P0, 16)); home = np.full((N, 8, R0), 65535)
    on = np.argsort(rng.random((N, 8, P0, 16)), axis=-1) < cnt[..., None]
    for q in range(N):
        for g in range(8):
            ix = np.flatnonzero(on[q, g])[:R0]; c = rng.permutation(R0); n = len(ix)
            post[q, g].reshape(-1)[ix] = c[:n]; home[q, g, c[:n]] = ix
            if n: home[q, g, c[n:]] = np.where(rng.random(R0 - n) < 0.5, 65535, ix[rng.integers(0, n, R0 - n)])
    cl = rng.integers(0, 24, (N, 8, P0)); pr = rng.integers(40, 200, (8, 24, 14)); gi = np.arange(8)[None, :, None]
    at = np.minimum(home >> 4, P0 - 1)
    kc = np.where(home == 65535, rng.integers(0, 24, home.shape), np.take_along_axis(cl, at, 2))
    x = np.clip(pr[gi, kc] + rng.integers(-40, 41, (N, 8, R0, 14)), 0, 255)
    cen = rng.integers(0, 256, (N, 8, P0, 16)); cen[..., :14] = pr[gi, cl] + rng.integers(-16, 17, (N, 8, P0, 14))
    m = N * P0; w = m // 24; od = np.argsort(cl.transpose(1, 0, 2).reshape(8, m) + rng.random((8, m)), axis=1); pos = np.argsort(od, axis=1)
    z = np.take_along_axis(od, ((pos[:, :, None] + rng.integers(-w, w + 1, (8, m, 16))) % m).reshape(8, 16 * m), 1)
    near = (P * (z // P0) + z % P0).reshape(8, N, P0, 16).transpose(1, 0, 2, 3)
    near = np.where(rng.random(near.shape) < 0.15, rng.integers(0, N * P, near.shape), near)
    sl = 16 * at[:, :, None, :] + rng.integers(0, 16, (N, 8, RO, R0))
    ab = np.take_along_axis(post.reshape(N, 8, 16 * P0), sl.reshape(N, 8, RO * R0), 2).reshape(N, 8, RO, R0); u = rng.random(ab.shape)
    ab = np.where(u < 0.3, np.arange(R0), np.where(u < 0.5, rng.integers(0, R, ab.shape), ab))
    return {"x": x, "home": home, "cen": cen, "post": post, "near": near, "ab": ab}
def pack(d):
    h = d["home"][..., None]; v = np.concatenate([d["x"], h >> 8, h & 255], axis=-1).astype(np.float32)
    def turn(a): return np.ascontiguousarray(a.transpose(0, 1, 3, 2)).reshape(N, 128, -1)
    return {"rec": turn(v).astype(BF), "post": turn(d["post"]).astype(np.int32), "cen": turn(d["cen"].astype(np.float32)).astype(BF), "near": turn(d["near"]).astype(np.int32),
            "absorb": np.stack([gtable(a.reshape(8, -1)) for a in d["ab"]])}
def setup_inputs(rng):
    return pack(world(rng, counts(rng, rng.choice(np.array([0.2, 0.4, 0.6]), (N, 8, 1)))))
def setup_inputs_room(rng):
    nf = rng.choice(np.array([0, 1, S - 1, S, S + 1, 3 * S]), (N, 8)); nf[0] = (S, S + 1, S - 1, 0, 1, 3 * S, S, 2 * S); nf[1, 0] = S
    fm = np.argsort(rng.random((N, 8, P0)), axis=-1) < nf[..., None]
    cnt = np.where(fm, rng.choice(np.array([L, 16]), fm.shape), np.where(rng.random(fm.shape) < 0.5, L - 1, rng.integers(1, L, fm.shape)))
    d = world(rng, cnt); d["x"][:, 0] = rng.integers(128, 256, (N, R0, 14)); d["cen"][:, 0, :, :14] = 0
    fp = np.flatnonzero(fm[1, 0]); fq = np.flatnonzero(~fm[0, 0])
    d["near"][0, 0, fq] = (P + fp[np.arange(len(fq)) % S])[:, None]
    return pack(d)
def setup_inputs_ties(rng):
    cnt = counts(rng, 0.5); cnt[:, :, :6] = 16
    d = world(rng, cnt); d["x"] = rng.integers(0, 3, (N, 8, R0, 14)); d["cen"][..., :14] = rng.integers(0, 3, (N, 8, P0, 14))
    d["x"][:, 0] = 7; d["cen"][:, 0, :, :14] = np.where(rng.random((N, P0, 1)) < 0.5, 7, rng.integers(5, 9, (N, P0, 14)))
    d["x"][:, 2] *= rng.random((N, R0, 1)) < 0.5; d["cen"][:, 2, :, :14] = rng.integers(5, 9, (N, P0, 14))
    d["ab"][:, :4] = np.arange(R0)
    d["near"][:, 1::2] = P * rng.integers(0, N, (N, 4, P0, 16)) + rng.integers(0, 6, (N, 4, P0, 16))
    return pack(d)
def setup_inputs_ends(rng):
    q = rng.permutation(N); cnt = counts(rng, 0.3); cnt[q[0]] = rng.integers(0, L, (8, P0)); cnt[q[1]] = L
    ch = rng.permutation(P0)[:5]; cnt[:, 3] = rng.integers(1, L, (N, P0)); cnt[:, 3, ch] = 16
    cnt[:, 4] = rng.integers(1, L, (N, P0)); cnt[:, 4, 0] = 16; cnt[:, 4, P0 - 1] = L
    d = world(rng, cnt); ab = d["ab"]; near = d["near"]; d["cen"][:, 3, :, :14] = 0
    ab[:, 1] = rng.choice(np.array([0, R0 - 1]), (N, RO, R0)); ab[:, 2] = rng.integers(R0, R, (N, RO, R0)); ab[:, 5] = rng.integers(0, R0, (N, 1, 1)); ab[:, 3] = np.arange(R0)
    near[:, 4] = P * rng.integers(0, N, (N, P0, 16)) + rng.choice(np.array([0, P0 - 1, P0, P - 1]), (N, P0, 16))
    near[:, 3] = P * rng.integers(0, N, (N, P0, 16)) + np.where(rng.random((N, P0, 16)) < 0.5, P0 + rng.integers(0, 5, (N, P0, 16)), ch[rng.integers(0, 5, (N, P0, 16))])
    for a in range(N):
        s = d["post"][a, 3, ch]; d["x"][a, 3, s[:, 0]] = 0; d["x"][a, 3, s[:, 1:].reshape(-1)] = rng.integers(200, 256, (75, 14))
    return pack(d)
def setup_inputs_sharp(rng):
    d = world(rng, counts(rng, 0.4)); E = N * S - 32; n = P0 - S; i = np.arange(n)
    tg = np.where(i < n - 32, i % E, E + i - (n - 32))
    for g in range(0, 8, 2):
        fs = [np.sort(rng.permutation(P0)[:S]) for q in range(N)]; to = np.concatenate([P * q + fs[q] for q in range(N)])
        for q in range(N):
            fp = fs[q]; fq = np.setdiff1d(np.arange(P0), fp); po = d["post"][q, g]
            dull = (rng.random(n) < 0.5) & ((i < E) | ((i >= 2 * E) & (i < n - 32)))
            z = int(np.flatnonzero(tg == q * S)[0]); dull[z] = False
            cnt = np.zeros(P0, np.int64); cnt[fp] = rng.integers(L, 16, S); cnt[fq] = rng.integers(1, 5, n); cnt[fq[z]] = 1
            key = rng.random((P0, 16)); key[fp, 0] = 2
            on = np.argsort(np.argsort(key, axis=1), axis=1) < cnt[:, None]
            ix = np.flatnonzero(on); m = len(ix); c = 1 + rng.permutation(R0 - 1); dead = c[m:]; low = dead[:len(dead) // 2]; high = dead[len(dead) // 2:]
            po[fp] = rng.choice(high, (S, 16)); po[fq] = rng.choice(low, (n, 16))
            po[on] = c[:m]; po[fq[z], int(np.argmax(on[fq[z]]))] = 0
            h = np.where(rng.random(R0) < 0.5, 65535, ix[rng.integers(0, m, R0)]); h[po[on]] = ix; d["home"][q, g] = h
            x = rng.integers(130, 201, (R0, 14)); x[low] = 0; x[high] = 255
            e = fp[::2]; x[po[e][on[e]]] = 0
            e = fp[1::2]; s = po[e][on[e]]; x[s] = rng.integers(0, 3, (len(s), 14))
            e = fq[~dull]; x[po[e][on[e]]] = 127
            d["x"][q, g] = x; d["cen"][q, g, fq, :14] = 255; d["ab"][q, g, 0] = np.arange(R0)
            d["near"][q, g, fq] = np.where(np.arange(16) < rng.integers(0, 15, (n, 1)), (P * q + fq)[:, None], to[tg][:, None])
    return pack(d)
def setup_inputs_spread(rng):
    d = world(rng, counts(rng, rng.random((N, 8, 1))))
    d["x"] = np.minimum((np.exp2(8 * rng.random((N, 8, R0, 1))) * rng.random((N, 8, R0, 14))).astype(np.int64), 255)
    d["cen"] = rng.integers(0, 256, (N, 8, P0, 16)) >> rng.integers(0, 8, (N, 8, P0, 1))
    d["near"] = rng.integers(0, N * P, (N, 8, P0, 16)); d["ab"] = rng.integers(0, R, (N, 8, RO, R0))
    return pack(d)
def check_inputs(d):
    bad = []
    for k, hi in (("rec", 255), ("cen", 255), ("post", R0 - 1), ("near", N * P - 1), ("absorb", R - 1)):
        v = np.asarray(d[k]).astype(np.float64)
        if not (np.min(v) >= 0 and np.max(v) <= hi) or np.any(v != np.floor(v)): bad.append("range of " + k)
    v = np.asarray(d["rec"]).astype(np.float64).reshape(N, 8, 16, R0); h = v[:, :, 14] * 256 + v[:, :, 15]
    if np.any((h >= 16 * P0) & (h != 65535)): bad.append("homes of rec")
    return bad
def reference(rec, post, cen, near, absorb):
    w = rec.astype(np.float32).astype(np.int32).reshape(N, 8, 16, R0)
    x = np.zeros((N, 8, 14, R), np.int32); x[..., :R0] = w[:, :, :14]
    home = np.full((N, 8, R), 65535, np.int64); home[..., :R0] = w[:, :, 14] * 256 + w[:, :, 15]
    po = np.zeros((N, 8, P, 16), np.int64); po[:, :, :P0] = post.reshape(N, 8, 16, P0).transpose(0, 1, 3, 2)
    ne = np.zeros((N, 8, P, 16), np.int64); ne[:, :, :P0] = near.reshape(N, 8, 16, P0).transpose(0, 1, 3, 2)
    ce = np.zeros((N, 8, 14, P), np.int32); ce[..., :P0] = cen.astype(np.float32).astype(np.int32).reshape(N, 8, 16, P0)[:, :, :14]
    al = np.stack([gentries(a) for a in absorb]).astype(np.int64).reshape(N, 8, RO, R0)
    for t in range(RO):
        new = P0 + S * t
        for q in range(N): x[q, :, :, :R0] = np.maximum(x[q, :, :, :R0], np.take_along_axis(x[q], al[q, :, t][:, None, :], 2))
        live = (np.take_along_axis(home, po.reshape(N, 8, 16 * P), 2) == np.arange(16 * P)).reshape(N, 8, P, 16)
        full = (np.add.reduce(live.astype(np.int64), axis=3) >= L).astype(np.int64)
        num = np.add.accumulate(full, axis=2) - full; sp = (full == 1) & (num < S)
        b = np.zeros((N, 8, S, 14), np.int32); row = np.zeros((N, 8, S), np.int64)
        for q in range(N):
            for g in range(8):
                for k, p in enumerate(np.flatnonzero(sp[q, g])):
                    f = new + k; ix = po[q, g, p].copy(); v = x[q, g][:, ix]; on = live[q, g, p]
                    va = v[:, np.argmax(on)]; da = np.add.reduce(np.abs(v - va[:, None]), axis=0)
                    vb = v[:, np.argmax(np.where(on, da, -1))]; db = np.add.reduce(np.abs(v - vb[:, None]), axis=0)
                    go = on & (db < da)
                    po[q, g, f] = ix; ne[q, g, f] = ne[q, g, p]; ce[q, g, :, p] = va; ce[q, g, :, f] = vb
                    home[q, g, ix[go]] = 16 * f + np.flatnonzero(go)
                    b[q, g, k] = vb; row[q, g, k] = np.argmin(go)
        tab = np.where(sp, num + S * np.arange(N)[:, None, None], -1).transpose(1, 0, 2).reshape(8, N * P)
        mov = np.full((N, 8, N * S), -1, np.int64)
        for q in range(N):
            tj = np.take_along_axis(tab, ne[q].reshape(8, 16 * P), 1).reshape(8, P, 16)
            tg = np.take_along_axis(tj, np.argmax(tj >= 0, axis=2)[:, :, None], 2)[:, :, 0]
            for g in range(8):
                Q = np.flatnonzero((tg[g] >= 0) & ~sp[q, g]); v = x[q, g][:, po[q, g, Q]]
                vb = b[:, g].reshape(N * S, 14).T[:, tg[g, Q]]
                gain = np.add.reduce(np.abs(v - ce[q, g][:, Q][:, :, None]), axis=0) - np.add.reduce(np.abs(v - vb[:, :, None]), axis=0)
                gain = np.where(live[q, g, Q], gain, 0); m = np.argmax(gain, axis=1); ok = np.any(gain > 0, axis=1)
                Q = Q[ok]; m = m[ok]; u, i = np.unique(tg[g, Q], return_index=True)
                mov[q, g, u] = po[q, g, Q[i], m[i]]
        for r in range(N):
            win = mov[r, :, r * S:(r + 1) * S].copy()
            for o, q in enumerate([a for a in range(N) if a != r]):
                c = mov[q, :, r * S:(r + 1) * S]; e = R0 + ((N - 1) * t + o) * S
                x[r, :, :, e:e + S] = np.where((c >= 0)[:, None, :], np.take_along_axis(x[q], np.maximum(c, 0)[:, None, :], 2), 0)
                gg, kk = np.nonzero(c >= 0); home[q, gg, c[gg, kk]] = 65535
                win = np.where((win < 0) & (c >= 0), e + np.arange(S), win)
            gg, kk = np.nonzero(win >= 0); m = row[r, gg, kk]
            home[r, gg, win[gg, kk]] = 16 * (new + kk) + m; po[r, gg, new + kk, m] = win[gg, kk]
    hh = np.stack([home >> 8, home & 255], axis=2)
    ya = np.concatenate([x[..., R0:], hh[..., R0:].astype(np.int32)], axis=2).reshape(N, 128, R - R0)
    return {"ypost": np.ascontiguousarray(po.transpose(0, 1, 3, 2)).reshape(N, 128, P).astype(np.float32),
            "yh": hh[..., :R0].reshape(N, 16, R0).astype(np.float32).astype(BF), "ya": ya.astype(np.float32).astype(BF)}

from concourse.bass import DstId, RemoteDMATransfer
from concourse.mybir import AluOpType as OP, AxisListType, ActivationFunctionType as AF

F, B, I, U, H16 = "float32", "bfloat16", "int32", "uint16", "float16"
_W = {
    B: "X0 4208 XB 3584 X1 3808 XA 112 H 4608 V 4864 W 4864 MC 4864 MB 4864 TN 4864 CEN 288 CE 320 TAB0 2688 TAB1 2688 L 448 LO 320 F0 320 F1 320 INC 320 LE 320 ZER 384 Z 320 BT0 128 BT1 128 MV0 128 MV1 128 "
       "VS 272 VSa 256 VSc 256 AD 256 BD 256 AA 256 BA 256 LS2 32 LT 32 RB 16 GE 32 GT 32 GS 16 LS16 16 CX1 304 CEX 304 CXT 384 E 2048 TB 24 TH 24 T8 384 BX1 128 BTX 128 X48 48 XT 384 TS 304 ZQ 2432 D0 2432 "
       "Y 192 VB 320 LOS 320 OHn 128 LN 128 FV 16 RB2 16 MVV0 128 MVV1 128 YA 224 YB 224 BO 128 TRI 128 ID 128 NID 128 U16 144 U14 144 UH 144 UC 144 WC 8 WB 8 WA 8 WV 8 SEL 8 LW 128 ZW 240 MKU 192 I16 16 EO 32 C31 16 "
       "IOB 128 C128 384 C15 384 C256 24 HV0 256 HV1 256 SA 128 SB1 128 SB2 128 RP 256 FST 128 BR0 512 BR1 512 TA 128 TB2 128 AH 224 AL 224 DA 224 DB 224 AR 3584 YR 4608 S1 128 S2 128 S3 128 S4 128 RM 1024",
    F: "PIf 320 SLOT 288 MA 320 pk 2 t2 1 SPf 16 CSf 16 LAf 16 LK 16 KL 16 KA 16 obf 1 g1 16 GO 16 RO 32 mx 1 T1 192 T2 192 T3 96 T4 48 hs 24 ok 24 OHm 128 PGm 256 W8 40 GLf 16 kk 7 sm 16 TT 96 TR 96 OH 16 OW 16 COL 48 "
       "IOT 256 IOS 288 G1 128 G2 136 G3 192 UF 144 L8f 12 C16 16 C16k 16 DGO 16 DMV 8 C7 7 CPf 320",
    I: "POI 288 ABI 448 NEI 320 NL0 32 NL1 32 kx 1 kr 1 ki 24 Ti 24 lo 24 IC 4 AI 224 PQ 288 PQ2 288",
    U: "PU 304 ABU 224 NU 304 pk2 2 NLu 8 SPu 16 CSu 16 LAu 16 obu 2 LBu 16 TLu 304 QTu 8 QTo 2 VLu 24 QLu 8 MVL 8 GLu 16 ARu 2 L8u 12 CU 304 PP 288",
    H16: "SC 2432",
}
_S = {}
for _d, _t in _W.items():
    _t = _t.split()
    for _i in range(0, len(_t), 2):
        _S[_t[_i]] = (int(_t[_i + 1]), _d)
_PS = ["PA", "PB", "PC", "PD", "PN", "PG", "PM0", "PM1"]
SCRATCH = {}
_PACK = {}
_n = {F: 0, I: 0, B: 0}
for _k in ("g1 KL KA LK GO RO LAf SPf CSf T3 T4 hs ok kk sm OH OW GLf W8 DGO DMV C7 C16 C16k obf t2 pk mx L8f TT TR G1 G2 G3 OHm kx kr ki Ti lo IC AI WC WB WA WV SEL I16 EO C31 GE GT LT LS2 RB RB2 "
           "TB TH C256 LW MKU BO TRI ID NID FST SA SB1 SB2 IOB UH UC U14 U16 ZW RP LS16 GS S1 S2 S3 S4 TA TB2 BX1 Y OHn LN FV AH AL DA DB VSc VSa AD BD AA BA Z").split():
    _w, _d = _S[_k]
    _PACK[_k] = ("PK" + _d, _n[_d])
    _n[_d] += (_w + 15) // 16 * 16
for _k, (_w, _d) in _S.items():
    if _k not in _PACK:
        SCRATCH[_k] = ("sbuf", [128, _w], _d)
for _d in (F, I, B):
    SCRATCH["PK" + _d] = ("sbuf", [128, _n[_d]], _d)
for _k in _PS:
    SCRATCH[_k] = ("psum", [128, 512], F)
_EX = ["a0", "b0", "c0", "a1", "b1", "c1"]
SEMAPHORES = ["cv", "ca", "ct", "cg"] + ["r" + e for e in _EX] + ["y" + e for e in _EX] + ["ls"] + ["d%d" % i for i in range(20)]


def bits(es):
    return sum(1 << e for e in es)


def parts(es, n):
    out, left = [], list(es)
    for i in range(n):
        k, s = n - i, 1
        while s * 2 <= (len(left) + k - 1) // k and s * 2 + (k - 1) <= len(left):
            s *= 2
        out.append(left[:s])
        left = left[s:]
    return out


def plan(r, T, topo):
    c = T.cores[r]
    direct = [d for d in range(len(T.cores)) if d != r and topo.may_write(c, T.cores[d])]
    cross = [d for d in range(len(T.cores)) if d != r and d not in direct]
    rel = [x for x in topo.cores_of(c) if x != c and topo.die(x) == topo.die(c) and T.rank_of(x) is None and all(topo.may_write(x, T.cores[d]) for d in cross)]
    rel = rel[:2] if cross else []
    return direct, [(x, cross[i::len(rel)]) for i, x in enumerate(rel)]


def masks_c(r, T, topo):
    direct, rel = plan(r, T, topo)
    c, last, on = T.cores[r], {}, {}
    if direct:
        for d, es in zip(direct, parts(topo.engines(c, T.cores[direct[0]]), len(direct))):
            last[d] = es
    ds = [(x, d) for x, q in rel for d in q]
    if ds:
        for (x, d), es in zip(ds, parts(topo.engines(c, ds[0][0]), len(ds))):
            on[d] = es
    for x, q in rel:
        for d, es in zip(q, parts(topo.engines(x, T.cores[q[0]]), len(q))):
            last[d] = es
    return last, on


def spot(T, r, d, t):
    a = (0 if t else 3584) + (r if r < d else r - 1) * 16
    return T["XA" if t else "X1"][:, a:a + 16]


def dst(topo, x, c):
    rid, pid = topo.addr(x, c)
    return DstId(rid=rid, pnc=pid)


def relay_program(g, core, T, topo):
    for r in range(len(T.cores)):
        direct, rel = plan(r, T, topo)
        for x, q in rel:
            if x == core:
                n = 0
                last, on = masks_c(r, T, topo)
                for ex in _EX:
                    k, t = ex[0], int(ex[1])
                    sr = T.sem["y" + ex]
                    if k == "c":
                        g.wait_ge(T.sem["r" + ex], sum(len(on[d]) for d in q))
                        g.remote_dma_fused([RemoteDMATransfer(dst_ids=[dst(topo, T.cores[d], core)], dma_engine_mask=bits(last[d]), remote_sem=sr, src=T["MV%d" % t][:, 16 * d:16 * d + 16],
                                                              dst=spot(T, r, d, t)) for d in q], local_sem=T.sem.ls)
                        n += sum(len(last[d]) for d in q)
                    else:
                        es = topo.engines(core, T.cores[q[0]])
                        ap = T["NL%d" % t][:, 4 * r:4 * r + 1] if k == "a" else T["BT%d" % t][:, 16 * r:16 * r + 16]
                        g.wait_ge(T.sem["r" + ex], len(topo.engines(T.cores[r], core)))
                        g.remote_dma_fused([RemoteDMATransfer(dst_ids=[dst(topo, T.cores[d], core) for d in q], dma_engine_mask=bits(es), remote_sem=sr, srcs=[ap], dsts=[ap for d in q])], local_sem=T.sem.ls)
                        n += len(es)
                g.wait_ge(T.sem.ls, n)


def rank_program(g, core, T, topo):
    r = T.rank_of(core)
    if r is None:
        relay_program(g, core, T, topo)
        return
    N = len(T.cores)
    E = {"v": g.vector, "a": g.scalar, "t": g.tensor, "g": g, "s": g.sync}
    CS = {"v": "cv", "a": "ca", "t": "ct", "g": "cg"}
    cnt = {}
    know = {e: {} for e in E}
    hist = {}
    ndma = [0]

    def v(n, a=0, b=None, st=1, p0=0, p1=128, ps=1):
        w = _S[n][0] if n in _S else (512 if n in _PS else T[n].shape[1])
        b = w if b is None else b
        if n in _PACK:
            nn, o = _PACK[n]
            return (nn, a + o, b + o, st, p0, p1, ps)
        return (n, a, b, st, p0, p1, ps)

    def ind(w, o):
        return ("IND", w, o)

    def ap(x):
        if x[0] == "IND":
            return ap(x[1]).indirect(ap(x[2]))
        n, a, b, st, p0, p1, ps = x
        if ps != 1:
            return T[n][p0:p1:ps, a:b]
        if p0 == 0 and p1 == 128:
            return T[n][:, a:b] if st == 1 else T[n][:, a:b:st]
        return T[n][p0:p1, a:b] if st == 1 else T[n][p0:p1, a:b:st]

    def regs(xs):
        out = []
        for x in xs:
            if isinstance(x, tuple):
                out += [x[1], x[2]] if x[0] == "IND" else [x]
        return out

    def deps(eng, outs, ins):
        need = {}
        for w, xs in ((True, outs), (False, ins)):
            for x in xs:
                ps = x[0] in _PS
                for h in hist.get(x[0], []):
                    if ps:
                        if h["e"] == eng and (eng == "t" or not (w or h["w"])):
                            continue
                    else:
                        if h["b"] <= x[1] or h["a"] >= x[2] or not (w or h["w"]):
                            continue
                        if h["st"] > 1 and h["st"] == x[3] and (h["a"] - x[1]) % x[3]:
                            continue
                    if need.get(h["s"], (0, None))[0] < h["n"]:
                        need[h["s"]] = (h["n"], h["k"])
        return need

    def waits(eng, need):
        for s, (n, k) in sorted(need.items(), key=lambda z: -len(z[1][1])):
            if know[eng].get(s, 0) < n:
                E[eng].wait_ge(T.sem[s], n)
                for a, b in k.items():
                    know[eng][a] = max(know[eng].get(a, 0), b)
                know[eng][s] = n

    def note(eng, sem, n, outs, ins, k):
        for w, xs in ((True, outs), (False, ins)):
            for x in xs:
                hs = hist.setdefault(x[0], [])
                if x[0] in _PS:
                    hs[:] = [h for h in hs if not (h["e"] == eng and h["w"] == w)]
                elif w and x[3] == 1 and x[4] == 0 and x[5] == 128:
                    hs[:] = [h for h in hs if not (h["a"] >= x[1] and h["b"] <= x[2])]
                elif not w:
                    hs[:] = [h for h in hs if not (h["e"] == eng and h["s"] == sem and not h["w"] and h["a"] >= x[1] and h["b"] <= x[2])]
                hs.append({"a": x[1], "b": x[2], "st": x[3], "w": w, "e": eng, "s": sem, "n": n, "k": k})

    def run(eng, fn, outs, ins, sem=None, inc=1):
        o, i = regs(outs), regs(ins)
        i = i + [x[2] for x in outs if x[0] == "IND"]
        waits(eng, deps(eng, o, i))
        s = sem or CS[eng]
        fn().then_inc(T.sem[s], inc)
        cnt[s] = cnt.get(s, 0) + inc
        note(eng, s, cnt[s], o, i, dict(know[eng]))

    def s_(x):
        return ap(x) if isinstance(x, tuple) else x

    def tt(o, a, b, op):
        run("v", lambda: g.vector.tensor_tensor(ap(o), ap(a), ap(b), op), [o], [a, b])

    def ts(o, a, s1, op0, s2=None, op1=None):
        if op1 is None:
            run("v", lambda: g.vector.tensor_scalar(ap(o), ap(a), s_(s1), None, op0), [o], [a, s1])
        else:
            run("v", lambda: g.vector.tensor_scalar(ap(o), ap(a), s_(s1), s_(s2), op0, op1), [o], [a, s1, s2])

    def tc(o, a):
        run("v", lambda: g.vector.tensor_copy(ap(o), ap(a)), [o], [a])

    def tr(o, a, op):
        run("v", lambda: g.vector.tensor_reduce(ap(o), ap(a), AxisListType.X, op), [o], [a])

    def vtr(o, a):
        run("v", lambda: g.vector.transpose(ap(o), ap(a)), [o], [a])

    def scan(o, a, b, init, op0, op1):
        run("v", lambda: g.vector.tensor_tensor_scan(ap(o), ap(a), ap(b), s_(init), op0, op1), [o], [a, b, init])

    def ms(o, c):
        run("v", lambda: g.vector.memset(ap(o), c), [o], [])

    def act(o, a, f=AF.Copy, bias=0.0, scale=1.0):
        run("a", lambda: g.scalar.activation(ap(o), ap(a), f, s_(bias), s_(scale)), [o], [a, bias, scale])

    def mm(o, l, x, start=True, stop=True):
        run("t", lambda: g.tensor.matmul(ap(o), ap(l), ap(x), start, stop), [o], [l, x])

    def iota(o, pat, base=0, ch=0):
        run("g", lambda: g.iota(ap(o), pat, base, ch, allow_small_or_imprecise_dtypes=True), [o], [])

    def dma(q, o, a):
        s = "d%d" % ndma[0]
        ndma[0] += 1
        run(q, lambda: (g.sync if q == "s" else g.scalar).dma_start(ap(o), ap(a)), [o], [a], s, 16)

    direct, rel = plan(r, T, topo)
    last, on = masks_c(r, T, topo)
    nls = [0]

    def bcast(ex, x):
        waits("g", deps("g", [], [x]))
        rs = [c for c, q in rel]
        if rs:
            es = topo.engines(core, rs[0])
            g.remote_dma_fused([RemoteDMATransfer(dst_ids=[dst(topo, c, core) for c in rs], dma_engine_mask=bits(es), remote_sem=T.sem["r" + ex], srcs=[ap(x)], dsts=[ap(x) for c in rs])], local_sem=T.sem.ls)
            nls[0] += len(es)
        if direct:
            es = topo.engines(core, T.cores[direct[0]])
            g.remote_dma_fused([RemoteDMATransfer(dst_ids=[dst(topo, T.cores[d], core) for d in direct], dma_engine_mask=bits(es), remote_sem=T.sem["y" + ex], srcs=[ap(x)], dsts=[ap(x) for d in direct])], local_sem=T.sem.ls)
            nls[0] += len(es)

    def movers(t):
        ex, nm = "c%d" % t, "MV%d" % t
        waits("g", deps("g", [], [v(nm)]))
        x_ = [RemoteDMATransfer(dst_ids=[dst(topo, x, core)], dma_engine_mask=bits(on[d]), remote_sem=T.sem["r" + ex], src=T[nm][:, 16 * d:16 * d + 16], dst=T[nm][:, 16 * d:16 * d + 16]) for x, q in rel for d in q]
        if x_:
            g.remote_dma_fused(x_, local_sem=T.sem.ls)
            nls[0] += sum(len(e) for e in on.values())
        x_ = [RemoteDMATransfer(dst_ids=[dst(topo, T.cores[d], core)], dma_engine_mask=bits(last[d]), remote_sem=T.sem["y" + ex], src=T[nm][:, 16 * d:16 * d + 16], dst=spot(T, r, d, t)) for d in direct]
        if x_:
            g.remote_dma_fused(x_, local_sem=T.sem.ls)
            nls[0] += sum(len(last[d]) for d in direct)

    def arrive(ex, regions):
        n = 0
        for q in range(N):
            if q != r:
                dq, rq = plan(q, T, topo)
                if ex[0] == "c":
                    n += len(masks_c(q, T, topo)[0][r])
                elif r in dq:
                    n += len(topo.engines(T.cores[q], T.cores[dq[0]]))
                else:
                    x, k = [(x, k) for x, k in rq if r in k][0]
                    n += len(topo.engines(x, T.cores[k[0]]))
        cnt["y" + ex] = n
        for x in regions:
            hist.setdefault(x[0], []).append({"a": x[1], "b": x[2], "st": x[3], "w": True, "e": "net", "s": "y" + ex, "n": n, "k": {}})

    def col(i):
        return v("COL", i, i + 1)

    (P_, M_, G_, G15, ODD, EVN, C13, K14, K15, C16_, UHC, WCC, R15, F15, I0, BC, LT8, GE8, K16, AR_, SAW, SBW, WBC, WAC, WVC, UCC, P1_, G14, WO, WO1, H18, H19) = range(32)
    TQ, TQB = 32, 40
    AS = AF.Identity

    dma("s", v("POI"), v("post"))
    dma("s", v("X0", 0, 1792), v("rec", 0, 1792))
    dma("a", v("X0", 1792, 3584), v("rec", 1792, 3584))
    dma("s", v("ABI"), v("absorb"))
    dma("a", v("CEN"), v("cen"))
    dma("s", v("XB"), v("rec"))
    dma("s", v("NEI", 0, 288), v("near"))
    ic = [v("IC", i, i + 1) for i in range(4)]
    iota(ic[0], [[0, 1]], 0, 1)
    iota(v("IOT"), [[1, 256]])
    iota(v("IOS"), [[16, 288]])
    iota(v("G1"), [[1, 8], [0, 16]])
    for q in range(8):
        iota(v("RM", 128 * q, 128 * q + 128), [[16, 8], [8, 2], [0, 8]], q)
    iota(v("I16"), [[1, 16]])
    iota(v("EO"), [[1, 2], [0, 16]])
    iota(v("C31"), [[-1, 16]], 31)
    iota(v("C16"), [[-1, 16]], 16)
    iota(v("C16k"), [[16, 16]])
    iota(v("E"), [[1, 128], [0, 16]])
    iota(v("TAB0"), [[0, 2688]], 4096)
    ts(ic[1], ic[0], 15, OP.bitwise_and)
    ts(ic[2], ic[0], 4, OP.arith_shift_right)
    ts(ic[3], ic[2], 1, OP.bitwise_and)
    for i in range(3):
        tc(col(i), ic[i])
    tc(col(ODD), ic[3])
    ts(col(G15), col(G_), 16, OP.mult, 15, OP.add)
    ts(col(EVN), col(ODD), -1, OP.mult, 1, OP.add)
    ts(col(C13), col(M_), 14, OP.is_lt)
    ts(col(K14), col(M_), 14, OP.is_equal)
    ts(col(K15), col(M_), 15, OP.is_equal)
    ts(col(UHC), col(K14), 256, OP.mult, col(K15), OP.add)
    ts(v("UH"), v("IOT", 0, 144), col(G15), OP.is_equal, col(UHC), OP.mult)
    ts(v("ID"), v("IOT", 0, 128), col(P_), OP.is_equal)
    ts(v("BO"), v("G1"), col(G_), OP.is_equal)
    ts(v("TRI"), v("IOT", 0, 128), col(P_), OP.is_ge)
    tt(v("TRI"), v("TRI"), v("BO"), OP.mult)
    tc(v("PU", 0, 288), v("POI"))
    for a, b in ((0, 96), (96, 208)):
        act(v("H", 16 * a, 16 * b), ind(v("X0", 0, 3584), v("PU", a, b)))
    ms(v("X0", 3584, 3808), 0)
    ms(v("X1", 3584, 3808), 0)
    ms(v("PIf", 288, 320), 0)
    ms(v("CPf", 288, 320), 0)
    ms(v("L"), 0)
    ms(v("CE", 288, 320), 0)
    tc(v("PIf", 0, 288), v("POI"))
    ts(v("SLOT"), v("IOS"), col(M_), OP.add)
    tc(v("H", 16 * 208, 4608), ind(v("X0", 0, 3584), v("PU", 208, 288)))
    tc(v("ABU"), v("ABI", 0, 224))
    for a, b in ((0, 96), (96, 208), (208, 288)):
        for m in range(16):
            mm(v("PA", a, b), v("UH", 15 - m, 143 - m), v("H", 16 * a + m, 16 * b, 16), m == 0, m == 15)
    ts(col(SAW), col(K14), 8, OP.mult, col(C13), OP.add)
    ts(col(SBW), col(K14), 16, OP.mult, col(C13), OP.add)
    ts(col(G14), col(G15), -1, OP.add)
    ts(col(P1_), col(P_), 1, OP.add)
    ts(v("TA"), v("ID"), col(C13), OP.mult)
    for nm, rr, wc in (("SA", G14, SAW), ("SB1", G15, SBW)):
        ts(v(nm), v("IOT", 0, 128), col(rr), OP.is_equal, col(wc), OP.mult)
        tt(v(nm), v(nm), v("TA"), OP.add)
    ts(v("TB2"), v("IOT", 0, 128), col(P1_), OP.is_equal)
    tt(v("TB2"), v("ID"), v("TB2"), OP.subtract)
    ts(v("SB2"), v("TB2"), col(K14), OP.mult)
    ms(v("ZER"), 0)
    ms(v("F0", 288, 304), 1)
    ms(v("F1", 304, 320), 1)
    ms(v("VS", 256, 272), 0)
    ts(col(R15), col(M_), 16, OP.mult, 15, OP.add)
    ts(col(C16_), col(C13), 16, OP.mult)
    act(v("CE", 0, 288), v("CEN"), AS, col(K14), col(C13))
    for a, b in ((0, 112), (112, 224)):
        tt(v("X1", 16 * a, 16 * b), ind(v("X0", 0, 3808), v("ABU", a, b)), v("XB", 16 * a, 16 * b), OP.max)

    def sums(src, w, mid, out, b1, b2):
        mm(v(b1, 0, w), v("SA"), v(src, 0, w))
        act(v(mid, 0, w), v(b1, 0, w))
        mm(v(b2, 0, w), v("SB1"), v(src, 0, w), True, False)
        mm(v(b2, 0, w), v("SB2"), v(mid, 0, w), False, True)
        act(v(out, 0, w), v(b2, 0, w))

    def nbs(t):
        return [128, 128, 32 + 16 * t]

    def centres(t):
        sums("CE", 288 + 16 * t, "CX1", "CEX", "PM0", "PM1")
        nb = nbs(t)
        for b in range(3):
            mm(v("PM0", 128 * b, 128 * b + 128, 1, 0, nb[b]), v("CEX", 128 * b, 128 * b + nb[b]), v("ID"))
        act(v("CXT", 0, 256), v("PM0", 0, 256))
        act(v("CXT", 256, 384, 1, 0, nb[2]), v("PM0", 256, 384, 1, 0, nb[2]))

    centres(0)

    def rows_open():
        ts(col(LT8), col(M_), 8, OP.is_lt)
        ts(col(GE8), col(M_), 8, OP.is_ge)
        ts(v("AI"), v("ABI", 224, 448), 255, OP.bitwise_and)
        tc(v("AL"), v("AI"))
        tt(v("AH"), v("ABI", 224, 448), v("AI"), OP.subtract)
        act(v("S1"), v("ID"), AF.Copy, 0.0, col(LT8))
        act(v("S4"), v("ID"), AF.Copy, 0.0, col(GE8))
        ts(v("S2"), v("IOT", 0, 128), -8, OP.add, col(P_), OP.is_equal)
        ts(v("S2"), v("S2"), col(LT8), OP.mult)
        ts(v("S3"), v("IOT", 0, 128), 8, OP.add, col(P_), OP.is_equal)
        ts(v("S3"), v("S3"), col(GE8), OP.mult)
        ts(v("RM"), v("RM"), col(P_), OP.is_equal)
        mm(v("PC", 0, 224), v("S1"), v("AH"), True, False)
        mm(v("PC", 0, 224), v("S2"), v("AL"), False, True)
        mm(v("PD", 0, 224), v("S3"), v("AH"), True, False)
        mm(v("PD", 0, 224), v("S4"), v("AL"), False, True)
        act(v("DA"), v("PC", 0, 224))
        act(v("DB"), v("PD", 0, 224))

    def rows(i, bank):
        for j in range(2):
            q = 2 * i + j
            mm(v(bank, 224 * j, 224 * j + 224), v("RM", 128 * (q % 8), 128 * (q % 8) + 128), v("DA" if q < 8 else "DB"))
        act(v("AR", 448 * i, 448 * i + 448), v(bank, 0, 448))

    def vgather(t, b):
        o = v("VW"[t], 2048 * b, 2048 * b + 16 * nbs(t)[b])
        if t == 0:
            act(o, ind(v("X1", 0, 3584), v("PU", 128 * b, 128 * b + nbs(t)[b])), AS, col(K14), col(C13))
        else:
            tt(o, ind(v("X1", 0, 3808), v("CU", 128 * b, 128 * b + nbs(t)[b])), v("V", 2048 * b, 2048 * b + 16 * nbs(t)[b]), OP.max)

    def count(t, a, b, fresh):
        Ft, P = "F%d" % t, 288 + 16 * t
        e = min(b, P)
        mm(v("PA", a, e), v("BO"), v("L", a, e))
        mm(v("PB", a, b), v("TRI"), v("L", a, b))
        ts(v(Ft, a, e), v("PA", a, e), 12, OP.is_ge)
        act(v("Z", a, b), v("PB", a, b), AF.Relu, 1.0, -1.0)
        mm(v("PB", a, b), v("BO"), v("Z", a, b))
        act(v("MA", a, b), v("PB", a, b))
        scan(v("INC", a, b), v(Ft, a, b), v("ZER", a, b), 0.0 if fresh else v("INC", a - 1, a), OP.add, OP.add)
        ts(v("LE", a, b), v("INC", a, b), col(M_), OP.is_le)
        tr(v("pk", 0, 1) if fresh else v("pk", 1, 2), v("LE", a, b), OP.add)
        if not fresh:
            tt(v("pk", 0, 1), v("pk", 0, 1), v("pk", 1, 2), OP.add)

    def numbers(t):
        P, k1 = 288 + 16 * t, v("pk", 0, 1)
        ts(v("pk2"), v("ZER", 0, 2), k1, OP.add)
        tc(v("SPu"), ind(v("PIf"), v("pk2", 0, 1)))
        if t == 1:
            tc(v("CSu"), ind(v("CPf"), v("pk2", 0, 1)))
        ts(v("t2"), k1, P, OP.is_ge, 2560 + 16 * r - 320 * r - P, OP.mult)
        ts(v("NL%d" % t, 4 * r, 4 * r + 1), v("t2"), k1, OP.add, 320 * r, OP.add)
        bcast("a%d" % t, v("NL%d" % t, 4 * r, 4 * r + 1))

    def kp(bank, x):
        mm(v(bank, 0, 16), v("ID"), v("C31"), True, False)
        for k in range(16):
            mm(v(bank, 0, 16), v("U16", 15 - k, 143 - k), v(x, 16 * k, 16 * k + 16), False, k == 15)

    def split_a(t):
        P, pk1 = 288 + 16 * t, v("pk2", 0, 1)
        if t == 0:
            act(v("VS", 0, 256), ind(v("X1", 0, 3584), v("SPu")), AS, col(K14), col(C13))
            tc(v("VSc"), ind(v("X1", 0, 3584), v("SPu")))
        else:
            act(v("VSa"), ind(v("X1", 0, 3808), v("SPu")), AS, col(K14), col(C13))
        tt(v("LAf"), ind(v("MA", 0, P + 16), pk1), v("C16k"), OP.add)
        tc(v("LAu"), v("LAf"))
        tt(v("LS2"), ind(v("L", 0, 320), v("pk2")), v("EO"), OP.mult)
        vtr(v("LT"), v("LS2"))
        tt(v("LK"), v("LT", 0, 16), v("LT", 16, 32), OP.add)
        if t == 1:
            tt(v("VS", 0, 256), ind(v("X1", 0, 3808), v("CSu")), v("VSa"), OP.max)
            tc(v("VSc"), v("VS", 0, 256))
        tt(v("AD"), ind(v("VS"), v("LAu")), v("VSc"), OP.subtract)
        tc(v("LO", 0, P), v("L", 0, P))
        tc(ind(v("LO", 0, P + 16), pk1), v("ZER", 0, 16))

    def split_b(t):
        tt(v("KL"), v("PC", 0, 16), v("LK"), OP.mult)
        tr(v("kx"), v("KL"), OP.max)
        ts(v("kr"), v("kx"), 15, OP.bitwise_and)
        ts(v("obu", 0, 1), v("kr"), -1, OP.mult, col(R15), OP.add)
        bt = v("BT%d" % t, 16 * r, 16 * r + 16)
        tc(bt, ind(v("VS"), v("obu", 0, 1)))
        bcast("b%d" % t, bt)

    def split_c(t):
        ts(v("obf"), v("kr"), -1, OP.mult, col(R15), OP.add)
        ts(v("RB"), v("I16"), v("obf"), OP.mult)
        mm(v("PD", 0, 16), v("BO"), v("RB"))
        tc(v("LBu"), v("PD", 0, 16))
        tt(v("BD"), ind(v("VS"), v("LBu")), v("VSc"), OP.subtract)
        act(v("KA"), v("PC", 0, 16))
        act(v("BA"), v("BD"), AF.Abs)
        kp("PD", "BA")

    def split_g():
        tt(v("g1"), v("PD", 0, 16), v("KA"), OP.is_lt)
        tt(v("GO"), v("g1"), v("LK"), OP.mult)

    def split_d(t):
        P, pk1 = 288 + 16 * t, v("pk2", 0, 1)
        tc(v("SPf"), ind(v("PIf"), pk1))
        act(v("GE", 0, 16), v("GO"), AF.Copy, 0.0, col(EVN))
        act(v("GE", 16, 32), v("GO"), AF.Copy, 0.0, col(ODD))
        vtr(v("GT"), v("GE"))
        tt(v("GS"), v("GT", 0, 16), v("GT", 16, 32), OP.add)
        tt(v("g1"), v("GO"), v("C16"), OP.mult)
        tt(v("KL"), v("C16"), v("g1"), OP.subtract)
        tr(v("mx"), v("KL"), OP.max)
        ts(v("RO", 0, 16), v("KL"), v("mx"), OP.is_equal, col(EVN), OP.mult)
        ts(v("RO", 16, 32), v("KL"), v("mx"), OP.is_equal, col(ODD), OP.mult)
        ts(v("obf"), v("mx"), -1, OP.mult, col(K16), OP.add)
        act(v("RB2"), v("I16"), AF.Copy, 0.0, v("obf"))
        mm(v("PC", 0, 16), v("BO"), v("RB2"))
        act(v("FV"), v("PC", 0, 16), AS, col(H18 + t), col(K15))
        act(v("MVV%d" % t, 16 * r, 16 * r + 16), v("FV"))
        tt(v("GLf"), v("SPf"), v("DGO"), OP.subtract)
        tt(v("GLf"), v("GLf"), v("GS"), OP.mult)
        tt(v("GLf"), v("GLf"), v("DGO"), OP.add)
        tc(v("GLu"), v("GLf"))
        if t == 0:
            tt(v("LS16"), ind(v("L", 0, 320), pk1), v("GS"), OP.subtract)
            tc(ind(v("L", 0, 320), pk1), v("LS16"))
            tt(v("RB"), v("AD", 0, 256, 16), v("VSc", 0, 256, 16), OP.add)
            tc(ind(v("CE"), pk1), v("RB"))
            tc(v("CE", P, P + 16), v("BT%d" % t, 16 * r, 16 * r + 16))
            tc(v("NU", P, P + 16), ind(v("NEI"), pk1))

    def go_homes(t):
        tc(ind(v("X0"), v("GLu")), v("HV%d" % t))

    def mcent(t, b, js=(0, 1, 2, 3)):
        nb = nbs(t)
        for j in js:
            n = min(512, 16 * nb[b] - 512 * j)
            if n > 0:
                c = 2048 * b + 512 * j
                pm = "PM%d" % (j % 2)
                kk = 128 if b < 2 else nb[b]
                mm(v(pm, 0, n), v("CXT", 128 * b, 128 * b + 128, 1, 0, kk), v("E", 512 * j, 512 * j + n, 1, 0, kk), True, b != 1)
                if b == 1:
                    mm(v(pm, 0, n), v("NID"), v("VW"[t], c, c + n), False, True)
                    act(v("MC", c, c + n), v(pm, 0, n), AF.Abs)
                else:
                    tt(v("MC", c, c + n), v(pm, 0, n), v("VW"[t], c, c + n), OP.max)

    def by_slot(bank, x, w, t, b):
        nb = nbs(t)
        for m in range(16):
            mm(v(bank, 24 * m + b, 24 * m + b + 22, 3, 0, nb[b]), v(x, 2048 * b + m, 2048 * b + 16 * nb[b], 16), v(w), False, False)

    def gain_open(t):
        nb = nbs(t)
        mm(v("PG", 0, 384), v("FST"), v("C15"), True, False)
        for b in range(3):
            for m in range(16):
                mm(v("PG", 24 * m + b, 24 * m + b + 22, 3, 0, nb[b]), v("LO", 128 * b, 128 * b + nb[b]), v("LW", 8 * m, 8 * m + 8), False, False)

    def close(bank):
        mm(v(bank, 0, 384), v("FST"), v("ZER"), False, True)

    def tree(bank, op, out):
        tc(v("T1"), v(bank, 192, 384))
        tt(v("T2"), v(bank, 0, 192), v("T1"), op)
        tt(v("T3"), v("T2", 0, 96), v("T2", 96, 192), op)
        tt(v("T4"), v("T3", 0, 48), v("T3", 48, 96), op)
        tt(out, v("T4", 0, 24), v("T4", 24, 48), op)

    def turn(x, n, out):
        for b in range(3):
            mm(v("PA", 128 * b, 128 * b + 128, 1, 0, n), v(x, b, 3 * n, 3), v("ID"))
        tc(v(out, 0, 384, 1, 0, n), v("PA", 0, 384, 1, 0, n))

    def table(t):
        arrive("a%d" % t, [v("NL%d" % t)])
        tc(v("NLu"), v("NL%d" % t, 0, 32, 4))
        tc(ind(v("TAB%d" % t), v("NLu")), v("IOB"))

    def near(t, b, vec=False):
        o, i = v("TN", 2048 * b, 2048 * b + 16 * nbs(t)[b]), ind(v("TAB%d" % t), v("NU", 128 * b, 128 * b + nbs(t)[b]))
        if vec:
            tc(o, i)
        else:
            act(o, i)

    def near_sums(t, bs):
        mm(v("PN", 0, 384), v("FST"), v("C128"), True, False)
        for b in bs:
            by_slot("PN", "TN", "SEL", t, b)
        close("PN")

    def targets(t):
        P = 288 + 16 * t
        tree("PN", OP.min, v("ki"))
        ts(v("Ti"), v("ki"), 127, OP.bitwise_and)
        tc(v("TB"), v("Ti"))
        sums("BT%d" % t, 128, "BX1", "BTX", "PC", "PD")
        turn("TB", 8, "T8")
        mm(v("PB", 0, P), v("RP", 0, 128, 1, 0, 8), v("T8", 0, P, 1, 0, 8))
        tc(v("TLu", 0, P), v("PB", 0, P))

    def far(t):
        nb = nbs(t)
        V = "VW"[t]
        by_slot("PG", "MC", "WV", t, 1)
        for j in range(5):
            if j < 4:
                c, br, pm = 2048 + 512 * j, "BR%d" % (j % 2), "PM%d" % (j % 2)
                act(v(br), ind(v("BTX"), v("TLu", 128 + 32 * j, 160 + 32 * j)))
                mm(v(pm), v("ID"), v(br), True, False)
                mm(v(pm), v("NID"), v(V, c, c + 512), False, True)
            if j > 0:
                c, pm = 1536 + 512 * j, "PM%d" % ((j - 1) % 2)
                act(v("MB", c, c + 512), v(pm), AF.Abs)
        for b in (2, 0):
            c, n = 2048 * b, 16 * nb[b]
            tt(v("MB", c, c + n), ind(v("BTX"), v("TLu", 128 * b, 128 * b + nb[b])), v(V, c, c + n), OP.max)
            if b == 2:
                ts(v("hs"), v("ki"), 4096, OP.is_lt)
                ts(v("ok"), v("TB"), -255, OP.add)
                tt(v("TH"), v("ok"), v("hs"), OP.mult)
        if t == 0:
            by_slot("PG", "MC", "WC", t, 2)
        by_slot("PG", "MB", "WB", t, 2)
        by_slot("PG", "MB", "WB", t, 0)
        by_slot("PG", "MB", "WA", t, 1)
        close("PG")

    def pick(t):
        P = 288 + 16 * t
        tree("PG", OP.max, v("ki"))
        ts(v("ok"), v("ki"), 262160, OP.is_ge)
        ts(v("lo"), v("ki"), 15, OP.bitwise_and)
        tt(v("X48", 24, 48), v("ok"), v("TH"), OP.mult)
        tc(v("X48", 0, 24), v("lo"))
        turn("X48", 16, "XT")
        mm(v("PB", 0, 304), v("RP", 128, 256, 1, 0, 16), v("XT", 0, 304, 1, 0, 16))
        act(v("TS"), v("PB", 0, 304))
        tt(v("Y"), ind(v("X48", 0, 24), v("L8u")), v("MKU"), OP.mult)
        mm(v("PD", 0, 24), v("ID"), v("C256"), True, False)
        for q in range(8):
            mm(v("PD", 0, 24), v("ZW", 112 - 16 * q, 240 - 16 * q), v("Y", 24 * q, 24 * q + 24), False, q == 7)
        mm(v("PC", 0, 304), v("RP", 0, 128, 1, 0, 16), v("XT", 0, 304, 1, 0, 16))
        ts(v("VLu"), v("PD", 0, 24), col(R15), OP.add)
        for q in range(6, 8):
            act(v("ZQ", 304 * q, 304 * q + 304), v("TS"), AF.Abs, col(TQB + q), 1000.0)
        act(v("VB", 0, P), ind(v("VW"[t], 0, 16 * P), v("VLu", 0, P // 16)))
        for q in range(6):
            ts(v("ZQ", 304 * q, 304 * q + 304), v("TS"), col(TQ + q), OP.not_equal, 1000, OP.mult)
        scan(v("SC"), v("D0"), v("ZQ"), 1000.0, OP.add, OP.min)
        ts(v("QTu"), v("SC", 303, 2432, 304), 303, OP.add, 304, OP.min)
        tc(v("MV%d" % t), ind(v("VB"), v("QTu")))
        act(v("LOS", 0, 304), v("PC", 0, 304))
        movers(t)

    def own(t):
        ex, x = v("W8", 0, 8), v("W8", 24, 32)
        ts(ex, v("SC", 303, 2432, 304), 0, OP.is_le)
        ts(v("OHm"), ind(v("LOS"), v("QTu")), col(F15), OP.is_equal)
        tt(v("PGm", 0, 128), ind(v("PIf"), v("QTu")), v("OHm"), OP.mult)
        if t == 0:
            ts(v("QTo", 0, 1), v("SC", 303 + 304 * r, 304 + 304 * r), 303, OP.add, 304, OP.min)
            ts(v("OHn"), ind(v("LOS"), v("QTu")), col(F15), OP.not_equal)
            tt(v("LN"), ind(v("L", 0, 320), v("QTu")), v("OHn"), OP.mult)
            ts(x, v("SC", 303, 2432, 304), 303 + 3744, OP.add)
            tt(x, x, v("DMV"), OP.subtract)
            tt(x, x, ex, OP.mult)
            tt(x, x, v("DMV"), OP.add)
            ts(v("QLu"), x, -3744, OP.add)
            tc(ind(v("L"), v("QLu")), v("LN"))
        ox = v("W8", r, r + 1)
        ts(v("sm", 0, 1), ox, -1, OP.mult, 1, OP.add)
        tt(v("sm", 1, 2), ox, own1(0), OP.mult)

    def own1(o):
        src = v("PGm", o + 16 * r, o + 16 * r + 16)
        ts(v("TT", 0, 16), src, col(EVN), OP.mult)
        ts(v("TT", 16, 32), src, col(ODD), OP.mult)
        vtr(v("TR", 0, 32), v("TT", 0, 32))
        tt(v("OH"), v("TR", 0, 16), v("TR", 16, 32), OP.add)
        tr(v("sm", 10, 11), v("OH"), OP.add)
        return v("sm", 10, 11)

    def own_c():
        tt(v("PGm", 128 + 16 * r, 144 + 16 * r), ind(v("CPf"), v("QTo", 0, 1)), v("OHm", 16 * r, 16 * r + 16), OP.mult)
        tt(v("sm", 8, 9), v("W8", r, r + 1), own1(128), OP.mult)

    def own_ids():
        for k in range(16):
            mm(v("PA", 0, 8), v("UF", 15 - k, 143 - k), v("PGm", k, 128, 16), k == 0, k == 15)

    def own2(t):
        ex, x = v("W8", 0, 8), v("W8", 24, 32)
        tc(v("W8", 8, 16), v("PA", 0, 8))
        tt(x, v("W8", 8, 16), v("DMV"), OP.subtract)
        tt(x, x, ex, OP.mult)
        tt(x, x, v("DMV"), OP.add)
        tc(v("MVL"), x)

    def mv_homes(t):
        tc(ind(v("X0"), v("MVL")), v("MVV%d" % t))

    def land(t):
        P = 288 + 16 * t
        nx, a0 = ("XA", 0) if t else ("X1", 3584)
        arrive("c%d" % t, [v(nx, a0, a0 + 112)])
        for k in range(16):
            mm(v("PC", 0, 7), v("U14", 15 - k, 143 - k), v(nx, a0 + k, a0 + 112, 16), k == 0, k == 15)
        tt(v("kk"), v("PC", 0, 7), v("C7"), OP.mult)
        km, hw, wo, w, wc = [v("sm", i, i + 1) for i in (2, 3, 4, 5, 9)]
        nown, ido, ox = v("sm", 0, 1), v("sm", 1, 2), v("W8", r, r + 1)
        tr(km, v("kk"), OP.max)
        ts(hw, km, ox, OP.max, 0, OP.is_gt)
        ts(v("TT", 0, 32), v("RO"), hw, OP.mult)
        ts(wo, km, -16, OP.mult, col(WO + t), OP.add)
        ts(w, wo, nown, OP.mult, ido, OP.add)
        ts(v("TT", 32, 64), v("TT", 0, 32), w, OP.mult)
        n = 64
        if t == 0:
            n = 96
            ts(wc, wo, nown, OP.mult, v("sm", 8, 9), OP.add)
            ts(v("TT", 64, 96), v("TT", 0, 32), wc, OP.mult)
        vtr(v("TR", 0, n), v("TT", 0, n))
        tt(v("OH"), v("TR", 0, 16), v("TR", 16, 32), OP.add)
        if t == 0:
            tt(v("L", P, P + 16), v("GS"), v("OH"), OP.add)
        for nm, pf, o in (("SPf", "PIf", 32), ("CSf", "CPf", 64)):
            if nm == "SPf" or t == 0:
                tt(v("OW"), v("TR", o, o + 16), v("TR", o + 16, o + 32), OP.add)
                tt(v("g1"), v(nm), v("OH"), OP.mult)
                tt(v("OW"), v(nm), v("OW"), OP.add)
                tt(v(pf, P, P + 16), v("OW"), v("g1"), OP.subtract)

    def land_home(t):
        hw, wo = v("sm", 3, 4), v("sm", 4, 5)
        ts(v("sm", 6, 7), hw, v("sm", 0, 1), OP.mult)
        tt(v("sm", 7, 8), wo, col(AR_), OP.subtract)
        ts(v("ARu", 0, 1), v("sm", 7, 8), v("sm", 6, 7), OP.mult, col(AR_), OP.add)
        tc(ind(v("X0"), v("ARu", 0, 1)), v("FV"))

    tt(v("L", 0, 288), v("PA", 0, 288), v("SLOT"), OP.is_equal)
    count(0, 0, 304, True)
    ts(v("EO"), v("EO"), col(ODD), OP.is_equal)
    numbers(0)
    iota(v("IOB"), [[1, 128]])
    iota(v("C128"), [[128, 16], [0, 24]])
    iota(v("C15"), [[-1, 16], [0, 24]], 15)
    iota(v("G2", 128, 136), [[1, 8]])
    iota(v("G2", 0, 128), [[1, 16], [16, 8]])
    iota(v("COL", TQ, TQ + 8), [[16, 8]], -255)
    ts(v("E"), v("E"), col(P_), OP.is_equal)
    ts(v("I16"), v("I16"), col(M_), OP.is_equal)
    ts(v("U16"), v("IOT", 0, 144), col(G15), OP.is_equal, col(C16_), OP.mult)
    split_a(0)
    vgather(0, 0)
    act(v("NID"), v("ID"), AF.Copy, 0.0, -1.0)
    act(v("AA"), v("AD"), AF.Abs)
    kp("PC", "AA")
    ms(v("NEI", 288, 320), 0)
    tc(v("NU", 0, 288), v("NEI", 0, 288))
    ms(v("FST"), 0)
    ms(v("FST", 0, 128, 1, 0, 1), 1)
    mcent(0, 0)
    split_b(0)
    vgather(0, 1)
    split_c(0)
    ts(col(I0), col(M_), 0, OP.is_equal)
    ts(col(WCC), col(C13), 48, OP.mult, -16, OP.add)
    ts(col(WBC), col(WCC), -1, OP.mult)
    ts(col(WAC), col(C13), -16, OP.mult)
    ts(col(WVC), col(C13), 16, OP.mult)
    for nm, wc in (("WC", WCC), ("WB", WBC), ("WA", WAC), ("WV", WVC), ("SEL", I0)):
        ts(v(nm), v("G2", 128, 136), col(G_), OP.is_equal, col(wc), OP.mult)
    ts(v("LW"), v("G2", 0, 128), col(P_), OP.is_equal, 262144, OP.mult)
    split_g()
    rows_open()
    vgather(0, 2)
    for i in range(4):
        rows(i, ("PN", "PG", "PC", "PD")[i])
    table(0)
    near(0, 1, True)
    mcent(0, 2)
    near(0, 0)
    near(0, 2)
    gain_open(0)
    by_slot("PG", "MC", "WC", 0, 0)
    near_sums(0, (1, 0, 2))
    mcent(0, 1, (0, 1))
    ts(v("PQ"), v("POI"), 15, OP.bitwise_and)
    ts(v("PQ2"), v("POI"), 4, OP.arith_shift_right)
    ts(v("PQ"), v("PQ"), 224, OP.mult)
    tt(v("PQ"), v("PQ"), v("PQ2"), OP.add)
    tc(v("PP"), v("PQ"))
    ts(v("RP", 0, 128), v("G1"), col(P_), OP.is_equal)
    ts(v("RP", 128, 256), v("G1"), 8, OP.add, col(P_), OP.is_equal)
    arrive("b0", [v("BT0")])
    targets(0)
    mcent(0, 1, (2, 3))
    for i in range(4, 8):
        rows(i, ("PC", "PD")[i % 2])
    iota(v("ZW"), [[1, 240]], -112)
    iota(v("G3"), [[0, 24], [1, 8]])
    iota(v("L8f"), [[2, 12]])
    iota(v("C256"), [[256, 24]])
    iota(v("DMV"), [[16, 8]], 4064)
    iota(v("C7"), [[-1, 7]], 7)
    iota(v("D0"), [[0, 2432]], -1)
    iota(v("D0", 0, 2432, 304), [[0, 8]], 5000)
    iota(v("VB"), [[0, 320]])
    iota(v("LOS", 304, 320), [[0, 16]])
    iota(v("MVV0"), [[0, 128]], 255)
    iota(v("MVV1"), [[0, 128]], 255)
    iota(v("TAB1"), [[0, 2688]], 4096)
    far(0)
    ts(col(K16), col(M_), 16, OP.mult, 16, OP.add)
    for t in range(2):
        ts(col(H18 + t), col(K14), 18 + t, OP.mult)
        ts(col(WO + t), col(M_), 3584 + 112 * t + 112, OP.add)
    ts(v("DGO"), v("C16k"), col(M_), OP.add, 3808, OP.add)
    split_d(0)
    ts(v("ZW"), v("ZW"), col(M_), OP.is_equal, -1, OP.mult)
    ts(v("MKU"), v("G3"), col(G_), OP.is_equal)
    ts(v("L8u"), v("L8f"), col(GE8), OP.add)
    ts(v("COL", TQ, TQ + 8), v("COL", TQ, TQ + 8), col(M_), OP.add)
    ts(v("COL", TQB, TQB + 8), v("COL", TQ, TQ + 8), -1000, OP.mult)
    ts(col(F15), col(M_), -1, OP.mult, 15, OP.add)
    act(v("YR", 0, 2048), ind(v("AR"), v("PP", 0, 128)))
    pick(0)
    act(v("YR", 2048, 4096), ind(v("AR"), v("PP", 128, 256)))
    act(v("YR", 4096, 4608), ind(v("AR"), v("PP", 256, 288)))
    act(v("X1", 0, 3584), v("X1", 0, 3584), AF.Copy, 0.0, col(C13))
    ts(v("DMV"), v("DMV"), col(M_), OP.add)
    for t in range(2):
        act(v("HV%d" % t), v("IOT"), AS, col(H18 + t), col(K15))
    ts(col(UCC), col(I0), 8, OP.add)
    ts(col(UCC), col(M_), col(UCC), OP.is_equal, col(I0), OP.add)
    ts(v("UC"), v("IOT", 0, 144), col(G15), OP.is_equal, col(UCC), OP.mult)
    ts(v("UF"), v("IOT", 0, 144), col(G15), OP.is_equal)
    ts(v("U14"), v("IOT", 0, 144), col(G15), OP.is_equal, col(K14), OP.mult)
    own(0)
    for a, b in ((0, 128), (128, 288)):
        for m in range(16):
            mm(v("PN", a, b), v("UC", 15 - m, 143 - m), v("YR", 16 * a + m, 16 * b, 16), m == 0, m == 15)
    tc(v("CPf", 0, 288), v("PN", 0, 288))
    tc(v("CSf"), ind(v("CPf"), v("pk2", 0, 1)))
    count(1, 0, 288, True)
    own_c()
    tc(v("CU", 0, 288), v("CPf", 0, 288))
    land(0)
    count(1, 288, 320, False)
    numbers(1)
    tc(v("PU", 288, 304), v("PIf", 288, 304))
    split_a(1)
    act(v("AA"), v("AD"), AF.Abs)
    kp("PC", "AA")
    centres(1)
    tc(v("CU", 288, 304), v("CPf", 288, 304))
    act(v("V", 4608, 4864), ind(v("X1", 0, 3808), v("PU", 288, 304)), AS, col(K14), col(C13))
    dma("s", v("ypost", 0, 304), v("PIf", 0, 304))
    split_b(1)
    split_c(1)
    vgather(1, 0)
    mcent(1, 0)
    own_ids()
    split_g()
    table(1)
    for b in range(3):
        near(1, b)
    vgather(1, 1)
    vgather(1, 2)
    mcent(1, 2)
    gain_open(1)
    by_slot("PG", "MC", "WC", 1, 0)
    by_slot("PG", "MC", "WC", 1, 2)
    near_sums(1, (0, 1, 2))
    mcent(1, 1, (0, 1))
    ts(col(AR_), col(M_), 4192, OP.add)
    ms(v("X0", 3584, 3808), 255)
    own2(0)
    go_homes(0)
    mv_homes(0)
    land_home(0)
    arrive("b1", [v("BT1")])
    targets(1)
    mcent(1, 1, (2, 3))
    far(1)
    split_d(1)
    go_homes(1)
    pick(1)
    own(1)
    own_ids()
    own2(1)
    mv_homes(1)
    dma("s", v("yh", 0, 3584, 1, 0, 16, 2), v("X0", 0, 3584, 1, 14, 128, 16))
    dma("a", v("yh", 0, 3584, 1, 1, 16, 2), v("X0", 0, 3584, 1, 15, 128, 16))
    ts(col(BC), col(C13), -1, OP.mult, 1, OP.add)
    land(1)
    dma("s", v("ypost", 304, 320), v("PIf", 304, 320))
    land_home(1)
    ts(v("YA", 0, 112), v("X1", 3584, 3696), col(C13), OP.mult)
    ts(v("YA", 112, 224), v("XA"), col(C13), OP.mult)
    ts(v("YB"), v("X0", 3584, 3808), col(BC), OP.mult)
    tt(v("YA"), v("YA"), v("YB"), OP.add)
    dma("a", v("ya"), v("YA"))
    cnt["ls"] = nls[0]
    waits("g", {s: (n, {}) for s, n in cnt.items() if n})
